import numpy as np
import ml_dtypes


def mxq(x, axis, fmt="e4m3"):
    dtype, down = {"e4m3": (ml_dtypes.float8_e4m3fn, 7), "e5m2": (ml_dtypes.float8_e5m2, 14)}[fmt]
    v = np.moveaxis(np.asarray(x, np.float32).astype(ml_dtypes.bfloat16).astype(np.float64), axis, -1)
    blocks = v.reshape(v.shape[:-1] + (-1, 32))
    amax = np.abs(blocks).max(-1, keepdims=True)
    byte = np.maximum(np.where(amax > 0, np.frexp(amax)[1] - 1 + 127, 0) - down, 1)
    scale = np.exp2(byte - 127.0)
    codes = (blocks / scale).astype(np.float32).astype(dtype).astype(np.float64)
    return np.moveaxis((codes * scale).reshape(v.shape), -1, axis)


WIDE = False


def mx_kscale(k):
    if not WIDE:
        return np.ones(k)
    levels = np.array([10, -10, 5, -5, 0])
    if k % 512:
        return np.exp2(np.random.permutation(np.resize(levels, k // 32))).repeat(32)
    a = np.empty((k // 512, 16))
    for p in range(k // 512):
        a[p, :8] = np.random.permutation(np.resize(levels, 8))
        for g in range(8):
            far = levels[np.abs(levels - a[p, g]) >= 10]
            a[p, g + 8] = far[np.random.randint(len(far))]
    return np.exp2(a.ravel()).repeat(32)


def f64(x):
    return np.asarray(x).astype(np.float64)


def striped(idx):
    return np.tile(idx.reshape(-1, 16).T, (8, 1)).astype(np.uint16)


def unstriped(offs):
    return offs[:16].T.reshape(-1).astype(np.int64)


E2M1 = np.array([0.0, 0.5, 1.0, 1.5, 2.0, 3.0, 4.0, 6.0, -0.0, -0.5, -1.0, -1.5, -2.0, -3.0, -4.0, -6.0])


def pack_weight(w, fmt):
    k, n = w.shape
    w = f64(np.asarray(w, np.float32).astype(ml_dtypes.bfloat16)).reshape(k // 32, 32, n)
    amax = np.abs(w).max(1)
    if fmt == "e4m3":
        byte = np.frexp(amax)[1] - 1 + 127 - 7
    else:
        mant, ex = np.frexp(amax / 6.0)
        byte = np.where(mant > 0.5, ex, ex - 1) + 127
    byte = np.clip(np.where(amax > 0, byte, 1), 1, 254)
    scaled = (w * np.exp2(127.0 - byte)[:, None, :]).reshape(k, n).astype(np.float32)
    by_word = np.ascontiguousarray(scaled.reshape(k // 512, 128, 4, n).transpose(0, 1, 3, 2))
    if fmt == "e4m3":
        words = by_word.astype(ml_dtypes.float8_e4m3fn).view(np.uint8)
    else:
        c = by_word.astype(ml_dtypes.float4_e2m1fn).view(np.uint8) & 0xF
        words = (c[..., 0::2] | (c[..., 1::2] << 4)).reshape(k // 512, 128, 2 * n)
    return np.ascontiguousarray(words), np.ascontiguousarray(byte.astype(np.uint8).reshape(k // 512, 16, n))


def unpack_weight(words, scales, fmt):
    g, _, n = scales.shape
    words = np.ascontiguousarray(words).reshape(g, 128, n, -1)
    if fmt == "e4m3":
        vals = words.view(ml_dtypes.float8_e4m3fn).astype(np.float64)
    else:
        nib = np.empty((g, 128, n, 4), np.uint8)
        nib[..., 0::2] = words & 0xF
        nib[..., 1::2] = words >> 4
        vals = E2M1[nib]
    vals = vals * np.repeat(np.exp2(scales.astype(np.float64) - 127.0), 8, axis=1)[..., None]
    return vals.transpose(0, 1, 3, 2).reshape(g * 512, n)


def gelu(v):
    return 0.5 * v * (1.0 + np.tanh(np.sqrt(2.0 / np.pi) * (v + 0.044715 * v**3)))


K, T, S, H, T3, S2, T2 = 1024, 2048, 1024, 1024, 2048, 512, 2048

def setup_inputs():
    n = np.random.standard_normal
    s = mx_kscale(K)[:, None]
    u = mx_kscale(H)[:, None]
    tab_words, tab_scales = pack_weight(n((K, T)) * s, "e4m3")
    tab2_words, tab2_scales = pack_weight(n((H, T3)) / np.sqrt(H) / u, "e4m3")
    w4_words, w4_scales = pack_weight(n((K, H)) / np.sqrt(K) / s * u.T, "e2m1")
    return {
        "tab_words": tab_words, "tab_scales": tab_scales,
        "offs": striped(np.random.permutation(T)[:S]),
        "tab2_words": tab2_words, "tab2_scales": tab2_scales,
        "offs2": striped(np.random.permutation(T3)[:S2]),
        "offs3": striped(np.random.permutation(T2)[:S]),
        "w4_words": w4_words, "w4_scales": w4_scales,
        "w1": (n((K, H)) / np.sqrt(K) / s * u.T).astype(np.float32),
        "boulder": (0.8 * n(S2)).astype(np.float32),
        "exposure": np.exp(0.4 * n((S2, S))).astype(np.float32),
        "wgo": np.exp(0.3 * n((128, S))).astype(np.float32),
        "page1": (0.7 * n((S2, T2))).astype(np.float32),
    }

def reference(tab_words, tab_scales, offs, tab2_words, tab2_scales, offs2, offs3,
              w4_words, w4_scales, w1, boulder, exposure, wgo, page1):
    v = unpack_weight(tab_words, tab_scales, "e4m3")[:, unstriped(offs)]
    v2 = unpack_weight(tab2_words, tab2_scales, "e4m3")[:, unstriped(offs2)]
    w4 = unpack_weight(w4_words, w4_scales, "e2m1")
    strength = w4.T @ v
    technique = mxq(f64(w1), 0, "e4m3").T @ v
    h = np.maximum(strength, technique)
    e = v2.T @ mxq(h, 0, "e4m3")
    d = np.tanh(e + f64(boulder)[:, None]) * f64(exposure)
    out = f64(page1).copy()
    out[:, unstriped(offs3)] = np.tile(f64(wgo), (S2 // 128, 1)) * d
    return out

from contextlib import ExitStack

import concourse.mybir as mybir

K, T, S, H, S2, T2 = 1024, 2048, 1024, 1024, 512, 2048
FLOPS = 2 * (2 * K * H * S + H * S2 * S)

F32 = mybir.dt.float32
BF16 = mybir.dt.bfloat16
I32 = mybir.dt.int32
U32 = mybir.dt.uint32
U16 = mybir.dt.uint16
U8 = mybir.dt.uint8
FP8X4 = mybir.dt.float8_e4m3fn_x4
FP4X4 = mybir.dt.float4_e2m1fn_x4
MULT = mybir.AluOpType.mult
MAX = mybir.AluOpType.max
TANH = mybir.ActivationFunctionType.Tanh

P = 128
HALF = 512


def tile_list_boulder_grade_panel_kernel(
    tc, tab_words, tab_scales, offs, tab2_words, tab2_scales, offs2, offs3,
    w4_words, w4_scales, w1, boulder, exposure, wgo, page1, out,
):
    nc = tc.nc
    with ExitStack() as ctx:
        lists = ctx.enter_context(tc.tile_pool(name="lists", bufs=1))
        keep = ctx.enter_context(tc.tile_pool(name="keep", bufs=1))
        stage = ctx.enter_context(tc.tile_pool(name="stage", bufs=2))
        psum = ctx.enter_context(tc.psum_pool(name="psum", bufs=1))

        def kept(name, cols, dtype):
            return keep.tile([P, cols], dtype, name=name, align_bytes=64)

        idx = lists.tile([P, S // 16], U16, name="idx")
        idx2 = lists.tile([P, S2 // 16], U16, name="idx2")
        idx3 = lists.tile([P, S // 16], U16, name="idx3")

        tab_sc = kept("tab_sc", T, U8)
        w4_sc_raw = kept("w4_sc_raw", 2 * H, U8)
        tab2_sc = kept("tab2_sc", T, U8)
        v_sc1 = kept("v_sc1", S, U8)
        nc.vector.memset(tab_sc[:].bitcast(I32), 0)
        nc.vector.memset(w4_sc_raw[:].bitcast(I32), 0)
        nc.vector.memset(v_sc1[:].bitcast(I32), 0)
        nc.vector.memset(tab2_sc[:].bitcast(I32), 0)

        nc.sync.dma_start(idx[:], offs)
        tab_w = [kept(f"tab_w{a}", T, U32) for a in range(2)]
        w4_raw = kept("w4_raw", 4 * H, U8)
        nc.sync.dma_start(
            w4_raw[:].bitcast(I32).rearrange("p (a n) -> p a n", a=2),
            w4_words.bitcast(I32).rearrange("a p n -> p a n"),
        )
        for q in range(4):
            nc.sync.dma_start(tab_sc[32 * q : 32 * q + 8, :].bitcast(I32), tab_scales[:, 4 * q : 4 * q + 4, :].bitcast(I32))
        for a in range(2):
            nc.sync.dma_start(tab_w[a][:].bitcast(I32), tab_words[a].rearrange("p n i -> p (n i)").bitcast(I32))
        for q in range(4):
            nc.sync.dma_start(
                w4_sc_raw[32 * q : 32 * q + 4, :].bitcast(I32).rearrange("r (a n) -> r a n", a=2),
                w4_scales[:, 4 * q : 4 * q + 4, :].bitcast(I32).rearrange("a r n -> r a n"),
            )
        w1_raw = {}

        def load_w1(a, b):
            w1_raw[a, b] = keep.tile([P, 4, HALF], F32, name=f"w1_raw{a}{b}", tag=f"wide{a}{b}")
            nc.sync.dma_start(
                w1_raw[a, b][:],
                w1[HALF * a : HALF * (a + 1), HALF * b : HALF * (b + 1)].rearrange("(p j) c -> p j c", j=4),
            )

        load_w1(0, 0)
        nc.sync.dma_start(idx2[:], offs2)

        v_w = {}

        def gather_v(a, jh):
            v_w[a, jh] = kept(f"v_w{a}{jh}", HALF, U32)
            nc.vector.tensor_copy(v_w[a, jh][:], tab_w[a][:].indirect(idx[:, 32 * jh : 32 * (jh + 1)]))

        w4_w = kept("w4_w", 4 * H, U8)
        for b in range(2):
            nc.scalar.copy(
                w4_w[:].bitcast(U16).rearrange("p (a b t m) -> p a b t m", a=2, b=2, t=4)[:, :, b],
                w4_raw[:].bitcast(U16).rearrange("p (a b m t) -> p a b t m", a=2, b=2, t=4)[:, :, b],
            )
        v_sc0 = kept("v_sc0", S, U8)
        nc.vector.tensor_copy(v_sc0[:], tab_sc[:].indirect(idx[:]))
        for q in range(4):
            nc.sync.dma_start(v_sc1[32 * q : 32 * q + 4, :].bitcast(I32), v_sc0[32 * q + 4 : 32 * q + 8, :].bitcast(I32))
        v_sc = [v_sc0, v_sc1]
        gather_v(0, 0)
        w4_sc = kept("w4_sc", 2 * H, U8)
        nc.vector.tensor_copy(
            w4_sc[:].rearrange("p (g t m) -> p g t m", g=4, t=4),
            w4_sc_raw[:].rearrange("p (g m t) -> p g t m", g=4, t=4),
        )
        gather_v(1, 0)
        gather_v(0, 1)
        gather_v(1, 1)

        load_w1(1, 0)
        load_w1(0, 1)
        load_w1(1, 1)
        for q in range(4):
            nc.sync.dma_start(tab2_sc[32 * q : 32 * q + 8, :].bitcast(I32), tab2_scales[:, 4 * q : 4 * q + 4, :].bitcast(I32))
        tab2_w = [kept(f"tab2_w{b}", T, U32) for b in range(2)]
        for b in range(2):
            nc.sync.dma_start(tab2_w[b][:].bitcast(I32), tab2_words[b].rearrange("p n i -> p (n i)").bitcast(I32))
        wgo_sb = kept("wgo_sb", S, F32)
        nc.sync.dma_start(wgo_sb[:], wgo)
        bias = kept("bias", 4, F32)
        with nc.allow_non_contiguous_dma(reason="boulder: one value a partition"):
            nc.sync.dma_start(bias[:], boulder.rearrange("(i p) -> p i", p=P))
        nc.sync.dma_start(idx3[:], offs3)
        factor = [kept(f"factor{i}", S, F32) for i in range(4)]
        for i in range(4):
            nc.sync.dma_start(factor[i][:], exposure[P * i : P * (i + 1), :])
        page = [kept(f"page{i}", T2, F32) for i in range(4)]
        for i in range(4):
            nc.sync.dma_start(page[i][:], page1[P * i : P * (i + 1), :])

        w1_w = {}
        w1_sc = {}

        def round_w1(a, b, copy):
            grouped = stage.tile([P, 4 * HALF], BF16, name="w1_grouped", align_bytes=64)
            copy(
                grouped[:].rearrange("p (t m j) -> p m j t", t=4, j=4),
                w1_raw[a, b][:].rearrange("p j (m t) -> p m j t", t=4),
            )
            return grouped

        def quantise_w1(a, b, grouped):
            w1_w[a, b] = kept(f"w1_w{a}{b}", HALF, U32)
            w1_sc[a, b] = kept(f"w1_sc{a}{b}", HALF, U8)
            nc.vector.quantize_mx(out=w1_w[a, b][:].bitcast(FP8X4), scales=w1_sc[a, b][:], in_=grouped[:])

        strength = {}

        def make_strength(b, jh):
            held = keep.tile([P, 2, 2, 256, 2], F32, name=f"strength{b}{jh}", tag=f"wide{jh}{b}")
            strength[b, jh] = held
            for c, u in ((0, 0), (0, 1), (1, 0), (1, 1)):
                jc = 2 * jh + c
                bank = psum.tile([P, 2, 256], F32, name="strength_bank", tag="by_scalar", bufs=5)
                for a in range(2):
                    for e in range(2):
                        col = H * a + HALF * b + P * (2 * u + e)
                        nc.tensor.matmul_mx(
                            out=bank[:, e, :],
                            lhsT=w4_w[:, 2 * col : 2 * (col + P)].bitcast(FP4X4),
                            lhsT_scale=w4_sc[:, col : col + P],
                            rhs=v_w[a, jh][:, 256 * c : 256 * (c + 1)].bitcast(FP8X4),
                            rhs_scale=v_sc[a][:, 256 * jc : 256 * (jc + 1)],
                            start=(a == 0 and e == 0),
                            stop=(a == 1 and e == 1),
                        )
                nc.scalar.copy(held[:, c, u], bank[:].rearrange("p e n -> p n e"))

        h_w = {}
        h_sc = {}

        def make_h(b, jh):
            h16 = stage.tile([P, 4 * HALF], BF16, name="h16", align_bytes=64)
            for n in range(4):
                j0 = HALF * jh + P * n
                bank = psum.tile([P, 4, P], F32, name="technique_bank", bufs=3)
                for a in range(2):
                    for t in range(4):
                        nc.tensor.matmul_mx(
                            out=bank[:, t, :],
                            lhsT=w1_w[a, b][:, P * t : P * (t + 1)].bitcast(FP8X4),
                            lhsT_scale=w1_sc[a, b][:, P * t : P * (t + 1)],
                            rhs=v_w[a, jh][:, P * n : P * (n + 1)].bitcast(FP8X4),
                            rhs_scale=v_sc0[4 * a :, j0 : j0 + P],
                            start=(a == 0 and t == 0),
                            stop=(a == 1 and t == 3),
                        )
                c, half = divmod(n, 2)
                nc.vector.tensor_tensor(
                    h16[:, HALF * n : HALF * (n + 1)].rearrange("p (n u e) -> p n u e", u=2, e=2),
                    bank[:].rearrange("p (u e) n -> p n u e", u=2),
                    strength[b, jh][:, c, :, P * half : P * (half + 1), :].rearrange("p u n e -> p n u e"),
                    MAX,
                )
            return h16

        def quantise_h(b, jh, h16):
            h_w[b, jh] = kept(f"h_w{b}{jh}", HALF, U32)
            h_sc[b, jh] = kept(f"h_sc{b}{jh}", HALF, U8)
            nc.vector.quantize_mx(out=h_w[b, jh][:].bitcast(FP8X4), scales=h_sc[b, jh][:], in_=h16[:])

        g00 = round_w1(0, 0, nc.scalar.copy)
        g10 = round_w1(1, 0, nc.vector.tensor_copy)
        quantise_w1(0, 0, g00)
        quantise_w1(1, 0, g10)
        make_strength(0, 0)
        h00 = make_h(0, 0)
        make_strength(0, 1)
        g01 = round_w1(0, 1, nc.scalar.copy)
        g11 = round_w1(1, 1, nc.scalar.copy)
        h01 = make_h(0, 1)
        quantise_h(0, 0, h00)
        quantise_w1(0, 1, g01)
        quantise_h(0, 1, h01)
        quantise_w1(1, 1, g11)
        make_strength(1, 0)

        v2_sc = kept("v2_sc", S2, U8)
        nc.vector.tensor_copy(v2_sc[:], tab2_sc[:].indirect(idx2[:]))
        v2_w = [kept(f"v2_w{b}", S2, U32) for b in range(2)]
        for b in range(2):
            nc.vector.tensor_copy(v2_w[b][:], tab2_w[b][:].indirect(idx2[:]))

        h10 = make_h(1, 0)
        make_strength(1, 1)
        quantise_h(1, 0, h10)

        for i in range(4):
            for jh in range(2):
                cols = slice(HALF * jh, HALF * (jh + 1))
                nc.gpsimd.tensor_tensor(factor[i][:, cols], factor[i][:, cols], wgo_sb[:, cols], MULT)

        score = {}

        def make_scores(i, jh):
            bank = psum.tile([P, HALF], F32, name="score_bank", tag="by_scalar", bufs=5)
            for b in range(2):
                nc.tensor.matmul_mx(
                    out=bank[:],
                    lhsT=v2_w[b][:, P * i : P * (i + 1)].bitcast(FP8X4),
                    lhsT_scale=v2_sc[4 * b :, P * i : P * (i + 1)],
                    rhs=h_w[b, jh][:].bitcast(FP8X4),
                    rhs_scale=h_sc[b, jh][:],
                    start=(b == 0),
                    stop=(b == 1),
                )
            score[i, jh] = stage.tile([P, HALF], F32, name="score", bufs=4)
            nc.scalar.activation(out=score[i, jh][:], in_=bank[:], func=TANH, bias=bias[:, i : i + 1])

        def put(i, jh):
            nc.vector.tensor_tensor(
                page[i][:].indirect(idx3[:, 32 * jh : 32 * (jh + 1)]),
                score[i, jh][:],
                factor[i][:, HALF * jh : HALF * (jh + 1)],
                MULT,
            )

        for i in range(2):
            make_scores(i, 0)
        h11 = make_h(1, 1)
        put(0, 0)
        quantise_h(1, 1, h11)
        put(1, 0)
        for i, jh in ((0, 1), (1, 1), (2, 0), (3, 0), (2, 1), (3, 1)):
            make_scores(i, jh)
            put(i, jh)
            if jh == 1:
                nc.sync.dma_start(out[P * i : P * (i + 1), :], page[i][:])
